import numpy as np
import ml_dtypes


def mxq(x, axis, fmt="e4m3"):
    dtype, down = {"e4m3": (ml_dtypes.float8_e4m3fn, 7), "e5m2": (ml_dtypes.float8_e5m2, 14)}[fmt]
    v = np.moveaxis(np.asarray(x, np.float32).astype(ml_dtypes.bfloat16).astype(np.float64), axis, -1)
    blocks = v.reshape(v.shape[:-1] + (-1, 32))
    amax = np.abs(blocks).max(-1, keepdims=True)
    byte = np.maximum(np.where(amax > 0, np.frexp(amax)[1] - 1 + 127, 0) - down, 1)
    scale = np.exp2(byte - 127.0)
    codes = (blocks / scale).astype(np.float32).astype(dtype).astype(np.float64)
    return np.moveaxis((codes * scale).reshape(v.shape), -1, axis)


WIDE = False


def mx_kscale(k):
    if not WIDE:
        return np.ones(k)
    levels = np.array([30, -30])
    if k % 512:
        return np.exp2(np.random.permutation(np.resize(levels, k // 32))).repeat(32)
    a = np.empty((k // 512, 16))
    for p in range(k // 512):
        a[p, :8] = np.random.permutation(np.resize(levels, 8))
        for g in range(8):
            far = levels[np.abs(levels - a[p, g]) >= 10]
            a[p, g + 8] = far[np.random.randint(len(far))]
    return np.exp2(a.ravel()).repeat(32)


BF16 = ml_dtypes.bfloat16


def bf(x):
    return np.asarray(x, np.float32).astype(BF16)


def f64(x):
    return np.asarray(x).astype(np.float64)


E2M1 = np.array([0.0, 0.5, 1.0, 1.5, 2.0, 3.0, 4.0, 6.0, -0.0, -0.5, -1.0, -1.5, -2.0, -3.0, -4.0, -6.0])


def pack_weight(w, fmt):
    k, n = w.shape
    w = f64(bf(w)).reshape(k // 32, 32, n)
    amax = np.abs(w).max(1)
    if fmt == "e4m3":
        byte = np.frexp(amax)[1] - 1 + 127 - 7
    else:
        mant, ex = np.frexp(amax / 6.0)
        byte = np.where(mant > 0.5, ex, ex - 1) + 127
    byte = np.clip(np.where(amax > 0, byte, 1), 1, 254)
    scaled = (w * np.exp2(127.0 - byte)[:, None, :]).reshape(k, n).astype(np.float32)
    by_word = np.ascontiguousarray(scaled.reshape(k // 512, 128, 4, n).transpose(0, 1, 3, 2))
    if fmt == "e4m3":
        words = by_word.astype(ml_dtypes.float8_e4m3fn).view(np.uint8)
    else:
        c = by_word.astype(ml_dtypes.float4_e2m1fn).view(np.uint8) & 0xF
        words = c[..., 0::2] | (c[..., 1::2] << 4)
    return np.ascontiguousarray(words), np.ascontiguousarray(byte.astype(np.uint8).reshape(k // 512, 16, n))


def unpack_weight(words, scales, fmt):
    g, p, n, _ = words.shape
    if fmt == "e4m3":
        vals = np.ascontiguousarray(words).view(ml_dtypes.float8_e4m3fn).astype(np.float64)
    else:
        nib = np.empty((g, p, n, 4), np.uint8)
        nib[..., 0::2] = words & 0xF
        nib[..., 1::2] = words >> 4
        vals = E2M1[nib]
    vals = vals * np.repeat(np.exp2(scales.astype(np.float64) - 127.0), 8, axis=1)[..., None]
    return vals.transpose(0, 1, 3, 2).reshape(g * 512, n)
def pack4(w):
    words, scales = pack_weight(w, "e2m1")
    return words.reshape(words.shape[0], 128, -1), scales


def unpack4(words, scales):
    return unpack_weight(words.reshape(words.shape[0], 128, -1, 2), scales, "e2m1")


M, K, F, R = 1024, 1024, 2048, 512


def setup_inputs():
    s = mx_kscale(K)
    t = mx_kscale(F)
    x = np.random.standard_normal((M, K)) * s
    a = np.random.standard_normal((K, F)) / np.sqrt(K) / s[:, None]
    a_words, a_scales = pack4(a)
    amp = (1 + 0.1 * np.random.standard_normal(F)) * t
    beta = np.random.standard_normal((F, R)) / np.sqrt(F) / t[:, None]
    lin = np.random.standard_normal((K, R)) / np.sqrt(K) / s[:, None]
    intercept = 0.3 * np.random.standard_normal(R)
    return {"x": bf(x), "a_words": a_words, "a_scales": a_scales, "amp": bf(amp),
            "beta": bf(beta), "lin": bf(lin), "intercept": bf(intercept)}


def reference(x, a_words, a_scales, amp, beta, lin, intercept):
    xq = mxq(f64(x), 1, "e4m3")
    z = xq @ unpack4(a_words, a_scales)
    h = np.square(z) * f64(amp)
    ridge = mxq(h, 1, "e5m2") @ mxq(f64(beta), 0, "e4m3")
    trend = xq @ mxq(f64(lin), 0, "e4m3")
    return ridge + trend + f64(intercept)

@@ -1,0 +1,378 @@
+from contextlib import ExitStack
+
+import concourse.mybir as mybir
+from concourse.masks import make_identity
+
+M, K, F, R = 1024, 1024, 2048, 512
+FLOPS = 2 * M * K * F + 2 * M * F * R + 2 * M * K * R
+
+F32 = mybir.dt.float32
+BF16 = mybir.dt.bfloat16
+I32 = mybir.dt.int32
+U32 = mybir.dt.uint32
+U8 = mybir.dt.uint8
+E4M3 = mybir.dt.float8_e4m3fn_x4
+E5M2 = mybir.dt.float8_e5m2_x4
+E2M1 = mybir.dt.float4_e2m1fn_x4
+ALU = mybir.AluOpType
+ACT = mybir.ActivationFunctionType
+
+P = 128
+PASS = 512
+KP = K // PASS
+G = F // PASS
+HALF = 512
+TINY = 2.0 ** -116
+
+
+def tile_projection_pursuit_regression_s9_kernel(tc, x, a_words, a_scales, amp, beta, lin, intercept, out):
+    nc = tc.nc
+    with ExitStack() as ctx:
+        keep = ctx.enter_context(tc.tile_pool(name="keep", bufs=1))
+        psum = ctx.enter_context(tc.psum_pool(name="psum", bufs=1))
+        ctx.enter_context(tc.manual_schedule())
+
+        def sb(name, shape, dtype):
+            return keep.tile(shape, dtype, name=name, tag=name, align_bytes=64)
+
+        def staged(name):
+            return keep.tile([P, 4 * HALF], BF16, name=name, tag="staged", bufs=3, align_bytes=64)
+
+        def bank(b, shape, name):
+            return psum.tile(shape, F32, name=name, tag="bank%d" % b)
+
+        ident = sb("ident", [P, P], F32)
+        sc_raw = sb("sc_raw", [P, KP, F], U8)
+        amp_rows = sb("amp_rows", [P, 4, P], F32)
+        amp_raw = sb("amp_raw", [G, PASS], BF16)
+        icpt = sb("icpt", [P, R], BF16)
+        root = sb("root", [P, 4, G], F32)
+        sgn = sb("sgn", [P, 4, G], F32)
+
+        x_raw, xq, xs = {}, {}, {}
+        for mh in range(2):
+            for kp in range(KP):
+                xq[mh, kp] = sb("xq%d%d" % (mh, kp), [P, HALF], U32)
+                xs[mh, kp] = sb("xs%d%d" % (mh, kp), [P, HALF], U8)
+        a_raw, aq, a_sc = {}, {}, {}
+        b_raw, b_int, bq, bs = {}, {}, {}, {}
+        l_raw, l_int, lq, ls = {}, {}, {}, {}
+        h_raw, h_int, hq, hs = {}, {}, {}, {}
+        x_ps, x_int, z_ps, o_ps = {}, {}, {}, {}
+        small = {}
+
+        def load_x(mh, kp, half):
+            t = sb("x_raw%d%d%d" % (mh, kp, half), [P, 2, PASS], BF16)
+            r0 = mh * HALF + half * 256
+            nc.sync.dma_start(out=t[:], in_=x[r0 : r0 + 256, kp * PASS : (kp + 1) * PASS].rearrange("(a p) k -> p a k", p=P))
+            x_raw[mh, kp, half] = t
+
+        def load_a(g):
+            t = sb("a_raw%d" % g, [P, KP, 2 * PASS], U8)
+            nc.sync.dma_start(
+                out=t[:].bitcast(I32),
+                in_=a_words[:, :, 2 * PASS * g : 2 * PASS * (g + 1)].rearrange("k p n -> p k n").bitcast(I32),
+            )
+            a_raw[g] = t
+
+        def load_scales():
+            for q in range(4):
+                nc.scalar.dma_start(
+                    out=sc_raw[32 * q : 32 * q + 4, :, :].bitcast(I32),
+                    in_=a_scales[:, 4 * q : 4 * q + 4, :].rearrange("k r n -> r k n").bitcast(I32),
+                )
+
+        def load_beta(g):
+            t = sb("b_raw%d" % g, [P, 4, R], BF16)
+            rows = beta[g * PASS : (g + 1) * PASS, :].rearrange("(j t i) r -> i j t r", t=4, i=4)
+            for i in range(4):
+                nc.sync.dma_start(out=t[i:P:4, :, :], in_=rows[i])
+            b_raw[g] = t
+
+        def load_lin(kp):
+            t = sb("l_raw%d" % kp, [P, 4, R], BF16)
+            nc.sync.dma_start(out=t[:], in_=lin[kp * PASS : (kp + 1) * PASS, :].rearrange("(p t) r -> p t r", t=4))
+            l_raw[kp] = t
+
+        def transpose_x(mh, kp, half):
+            ps = bank(4 + 2 * kp + half, [P, 2, 2, P], "x_ps%d%d%d" % (mh, kp, half))
+            words = x_raw[mh, kp, half][:].bitcast(F32)
+            for a in range(2):
+                for u in range(2):
+                    nc.tensor.transpose(ps[:, a, u, :], words[:, a, u : PASS // 2 : 2], ident[:])
+            x_ps[mh, kp, half] = ps
+
+        def copy_x(mh, kp, half, copy):
+            t = sb("x_int%d%d%d" % (mh, kp, half), [P, 1024], BF16)
+            copy(
+                out=t[:].bitcast(F32).rearrange("p (a m u) -> p a m u", a=2, u=2),
+                in_=x_ps[mh, kp, half][:].rearrange("p a u m -> p a m u"),
+            )
+            x_int[mh, kp, half] = t
+
+        def quant_x(mh, kp, half):
+            cols = slice(256 * half, 256 * (half + 1))
+            nc.vector.quantize_mx(out=xq[mh, kp][:, cols].bitcast(E4M3), scales=xs[mh, kp][:, cols], in_=x_int[mh, kp, half][:])
+
+        def sort_a(g):
+            t = sb("aq%d" % g, [P, KP, 2 * PASS], U8)
+            nc.vector.tensor_copy(
+                out=t[:].bitcast(I32).rearrange("p k (t j w) -> p k t j w", t=4, w=2),
+                in_=a_raw[g][:].bitcast(I32).rearrange("p k (j t w) -> p k t j w", t=4, w=2),
+            )
+            aq[g] = t
+
+        def sort_scales(g):
+            t = sb("a_sc%d" % g, [P, KP, PASS], U8)
+            nc.vector.tensor_copy(
+                out=t[:].bitcast(I32).rearrange("p k (t j) -> p k t j", t=4),
+                in_=sc_raw[:, :, PASS * g : PASS * (g + 1)].bitcast(I32).rearrange("p k (j t) -> p k t j", t=4),
+            )
+            a_sc[g] = t
+
+        def interleave(copy, dst, src, c0, c1):
+            copy(
+                out=dst[:, 4 * c0 : 4 * c1].rearrange("p (c i t) -> p c t i", i=4, t=4),
+                in_=src[:, :, c0:c1].rearrange("p t (c i) -> p c t i", i=4),
+            )
+
+        def sign_beta(g):
+            for t in range(4):
+                nc.vector.tensor_scalar(b_raw[g][:, t, :], b_raw[g][:, t, :], sgn[:, t, g : g + 1], None, ALU.mult)
+
+        def int_beta(g):
+            b_int[g] = staged("b_int%d" % g)
+            interleave(nc.vector.tensor_copy, b_int[g], b_raw[g], 0, R)
+
+        def quant_beta(g):
+            bq[g] = sb("bq%d" % g, [P, R], U32)
+            bs[g] = sb("bs%d" % g, [P, R], U8)
+            nc.vector.quantize_mx(out=bq[g][:].bitcast(E4M3), scales=bs[g][:], in_=b_int[g][:])
+
+        def int_lin(kp, half):
+            if half == 0:
+                l_int[kp] = sb("l_int%d" % kp, [P, 4 * R], BF16)
+            interleave(nc.scalar.copy, l_int[kp], l_raw[kp], 256 * half, 256 * (half + 1))
+
+        def quant_lin(kp):
+            lq[kp] = sb("lq%d" % kp, [P, R], U32)
+            ls[kp] = sb("ls%d" % kp, [P, R], U8)
+            nc.vector.quantize_mx(out=lq[kp][:].bitcast(E4M3), scales=ls[kp][:], in_=l_int[kp][:])
+
+        def z_pass(s, t, kp):
+            mh, g = divmod(s, G)
+            if kp == 0:
+                z_ps[s, t] = bank(t, [P, HALF], "z%d%d" % (s, t))
+            nc.tensor.matmul_mx(
+                out=z_ps[s, t][:],
+                lhsT=aq[g][:, kp, 256 * t : 256 * (t + 1)].bitcast(E2M1),
+                lhsT_scale=a_sc[g][:, kp, P * t : P * (t + 1)],
+                rhs=xq[mh, kp][:].bitcast(E4M3),
+                rhs_scale=xs[mh, kp][:],
+                start=(kp == 0),
+                stop=(kp == KP - 1),
+            )
+
+        def square(s, t):
+            g = s % G
+            if t == 0:
+                h_raw[s] = sb("h_raw%d" % s, [P, 4, HALF], BF16)
+            nc.scalar.activation(out=h_raw[s][:, t, :], in_=z_ps[s, t][:], func=ACT.Square, scale=root[:, t, g : g + 1])
+
+        def z_group(s):
+            for t in range(4):
+                for kp in range(KP):
+                    z_pass(s, t, kp)
+                square(s, t)
+
+        def int_h(s, c0=0, c1=HALF, copy=nc.vector.tensor_copy):
+            if c0 == 0:
+                h_int[s] = staged("h_int%d" % s)
+            interleave(copy, h_int[s], h_raw[s], c0, c1)
+
+        def quant_h(s, c0=0, c1=HALF):
+            if c0 == 0:
+                hq[s] = sb("hq%d" % s, [P, HALF], U32)
+                hs[s] = sb("hs%d" % s, [P, HALF], U8)
+            nc.vector.quantize_mx(out=hq[s][:, c0:c1].bitcast(E5M2), scales=hs[s][:, c0:c1], in_=h_int[s][:, 4 * c0 : 4 * c1])
+
+        done = {}
+
+        def out_pass(mh, a, lhs, lhs_scale, rhs, rhs_scale):
+            n = done.get((mh, a), 0)
+            if n == 0:
+                o_ps[mh, a] = bank(4 + a, [P, R], "o%d%d" % (mh, a))
+            nc.tensor.matmul_mx(
+                out=o_ps[mh, a][:], lhsT=lhs, lhsT_scale=lhs_scale, rhs=rhs, rhs_scale=rhs_scale,
+                start=(n == 0), stop=(n == KP + G - 1),
+            )
+            done[mh, a] = n + 1
+
+        def ridge(s, a):
+            mh, g = divmod(s, G)
+            cols = slice(P * a, P * (a + 1))
+            out_pass(mh, a, hq[s][:, cols].bitcast(E5M2), hs[s][:, cols], bq[g][:].bitcast(E4M3), bs[g][:])
+
+        def trend(mh, a, kps=range(KP)):
+            cols = slice(P * a, P * (a + 1))
+            for kp in kps:
+                out_pass(mh, a, xq[mh, kp][:, cols].bitcast(E4M3), xs[mh, kp][:, cols], lq[kp][:].bitcast(E4M3), ls[kp][:])
+
+        def finish(mh, a, parts=1):
+            r0 = mh * HALF + P * a
+            w = R // parts
+            for c in range(parts):
+                y = sb("y%d%d%d" % (mh, a, c), [P, w], F32)
+                cols = slice(w * c, w * (c + 1))
+                nc.vector.tensor_tensor(out=y[:], in0=o_ps[mh, a][:, cols], in1=icpt[:, cols], op=ALU.add)
+                nc.sync.dma_start(out=out[r0 : r0 + P, cols], in_=y[:])
+
+        nc.vector.memset(sc_raw[:].bitcast(I32), 0)
+        make_identity(nc, ident[:])
+        nc.vector.memset(amp_rows[:], 0.0)
+        nc.sync.dma_start(out=amp_raw[:], in_=amp.rearrange("(g f) -> g f", g=G))
+        load_x(0, 0, 0)
+        load_x(0, 0, 1)
+        load_a(0)
+        load_scales()
+        load_x(0, 1, 0)
+        load_x(0, 1, 1)
+        load_lin(0)
+        load_a(1)
+        load_beta(0)
+        load_x(1, 0, 0)
+        load_x(1, 0, 1)
+        load_a(2)
+        load_x(1, 1, 0)
+        load_x(1, 1, 1)
+        load_a(3)
+        load_beta(1)
+        load_lin(1)
+        load_beta(2)
+        load_beta(3)
+        nc.sync.dma_start(out=icpt[:], in_=intercept.partition_broadcast(P))
+
+        nc.vector.tensor_copy(
+            out=amp_rows[0:G, :, :].rearrange("g t (j i) -> g t j i", i=4),
+            in_=amp_raw[:].rearrange("g (j t i) -> g t j i", t=4, i=4),
+        )
+        amp_ps = bank(3, [P, 4, P], "amp_ps")
+        for t in range(4):
+            nc.tensor.transpose(amp_ps[:, t, :], amp_rows[:, t, :], ident[:])
+        for name in ("val", "mag", "guess", "inv", "neg", "quot", "sgn0", "halfroot"):
+            small[name] = sb(name, [P, 4, G], F32)
+        val = small["val"][:]
+        nc.vector.tensor_copy(out=val, in_=amp_ps[:, :, 0:G])
+        transpose_x(0, 0, 0)
+        transpose_x(0, 0, 1)
+        transpose_x(0, 1, 0)
+        transpose_x(0, 1, 1)
+        nc.vector.scalar_tensor_tensor(out=small["mag"][:], in0=val, scalar=-1.0, in1=val, op0=ALU.mult, op1=ALU.max)
+        nc.scalar.activation(out=small["guess"][:], in_=small["mag"][:], func=ACT.Sqrt, bias=TINY)
+        copy_x(0, 0, 0, nc.vector.tensor_copy)
+        sort_a(0)
+        quant_x(0, 0, 0)
+        copy_x(0, 0, 1, nc.vector.tensor_copy)
+        sort_scales(0)
+        quant_x(0, 0, 1)
+        copy_x(0, 1, 0, nc.scalar.copy)
+        copy_x(0, 1, 1, nc.scalar.copy)
+        nc.vector.tensor_scalar(small["neg"][:], val, 0.0, None, ALU.is_lt)
+        nc.vector.reciprocal(out=small["inv"][:], in_=small["guess"][:])
+        nc.vector.scalar_tensor_tensor(out=small["sgn0"][:], in0=val, scalar=0.0, in1=small["neg"][:], op0=ALU.is_gt, op1=ALU.subtract)
+        nc.vector.scalar_tensor_tensor(out=small["quot"][:], in0=val, scalar=0.5, in1=small["inv"][:], op0=ALU.mult, op1=ALU.mult)
+        nc.vector.scalar_tensor_tensor(out=small["halfroot"][:], in0=small["guess"][:], scalar=0.5, in1=small["sgn0"][:], op0=ALU.mult, op1=ALU.mult)
+        quant_x(0, 1, 0)
+        nc.vector.tensor_tensor(out=root[:], in0=small["halfroot"][:], in1=small["quot"][:], op=ALU.add)
+        quant_x(0, 1, 1)
+        nc.vector.tensor_scalar(sgn[:], small["neg"][:], -2.0, 1.0, ALU.mult, ALU.add)
+
+        int_lin(0, 0)
+        int_lin(0, 1)
+        for t in range(4):
+            z_pass(0, t, 0)
+        for t in range(4):
+            z_pass(0, t, 1)
+            square(0, t)
+
+        def ridges(s):
+            for a in range(4):
+                ridge(s, a)
+
+        def trends(mh, kp):
+            for a in range(4):
+                trend(mh, a, [kp])
+
+        sort_a(1)
+        sort_scales(1)
+        z_group(1)
+        sign_beta(0)
+        sort_scales(2)
+        int_beta(0)
+        sort_a(2)
+        quant_beta(0)
+        for half in range(2):
+            transpose_x(1, 0, half)
+            copy_x(1, 0, half, nc.scalar.copy)
+        z_group(2)
+        sort_scales(3)
+        int_h(0)
+        sort_a(3)
+        quant_h(0)
+        quant_lin(0)
+        sign_beta(1)
+        quant_x(1, 0, 0)
+        quant_x(1, 0, 1)
+        int_beta(1)
+        for half in range(2):
+            transpose_x(1, 1, half)
+            copy_x(1, 1, half, nc.scalar.copy)
+        z_group(3)
+        int_h(1)
+        quant_beta(1)
+        quant_x(1, 1, 0)
+        quant_x(1, 1, 1)
+        quant_h(1)
+        ridges(0)
+        trends(0, 0)
+        int_lin(1, 0)
+        int_lin(1, 1)
+        z_group(4)
+        sign_beta(2)
+        int_h(2)
+        int_beta(2)
+        quant_h(2)
+        quant_lin(1)
+        quant_beta(2)
+        ridges(1)
+        trends(0, 1)
+        z_group(5)
+        sign_beta(3)
+        int_h(3)
+        int_beta(3)
+        quant_h(3)
+        int_h(4)
+        quant_beta(3)
+        ridges(2)
+        z_group(6)
+        ridges(3)
+        quant_h(4)
+        int_h(5)
+        z_group(7)
+        finish(0, 0)
+        quant_h(5)
+        finish(0, 1)
+        finish(0, 2)
+        finish(0, 3)
+        int_h(6)
+        trends(1, 0)
+        trends(1, 1)
+        ridges(4)
+        ridges(5)
+        int_h(7)
+        quant_h(6)
+        quant_h(7)
+        for a in range(4):
+            ridge(6, a)
+            ridge(7, a)
+            finish(1, a)

@@ -42,9 +42,11 @@ def tile_projection_pursuit_regression_s9_kernel(tc, x, a_words, a_scales, amp, 
             return psum.tile(shape, F32, name=name, tag="bank%d" % b)
 
         ident = sb("ident", [P, P], F32)
-        sc_raw = sb("sc_raw", [P, KP, F], U8)
-        amp_rows = sb("amp_rows", [P, 4, P], F32)
-        amp_raw = sb("amp_raw", [G, PASS], BF16)
+        sc_first = sb("sc_first", [P, KP, PASS], U8)
+        sc_rest = sb("sc_rest", [P, KP, F - PASS], U8)
+        amp_raw = sb("amp_raw", [P, PASS], BF16)
+        amp_rows = sb("amp_rows", [P, PASS], BF16)
+        amp_cols = sb("amp_cols", [P, PASS], BF16)
         icpt = sb("icpt", [P, R], BF16)
         root = sb("root", [P, 4, G], F32)
         sgn = sb("sgn", [P, 4, G], F32)
@@ -61,11 +63,14 @@ def tile_projection_pursuit_regression_s9_kernel(tc, x, a_words, a_scales, amp, 
         x_ps, x_int, z_ps, o_ps = {}, {}, {}, {}
         small = {}
 
-        def load_x(mh, kp, half):
-            t = sb("x_raw%d%d%d" % (mh, kp, half), [P, 2, PASS], BF16)
+        def load_x(mh, kp, half, halves=1):
+            t = sb("x_raw%d%d%d" % (mh, kp, half), [P, 2 * halves, PASS], BF16)
             r0 = mh * HALF + half * 256
-            nc.sync.dma_start(out=t[:], in_=x[r0 : r0 + 256, kp * PASS : (kp + 1) * PASS].rearrange("(a p) k -> p a k", p=P))
-            x_raw[mh, kp, half] = t
+            nc.sync.dma_start(
+                out=t[:], in_=x[r0 : r0 + 256 * halves, kp * PASS : (kp + 1) * PASS].rearrange("(a p) k -> p a k", p=P)
+            )
+            for n in range(halves):
+                x_raw[mh, kp, half + n] = t[:, 2 * n : 2 * n + 2, :]
 
         def load_a(g):
             t = sb("a_raw%d" % g, [P, KP, 2 * PASS], U8)
@@ -75,11 +80,11 @@ def tile_projection_pursuit_regression_s9_kernel(tc, x, a_words, a_scales, amp, 
             )
             a_raw[g] = t
 
-        def load_scales():
-            for q in range(4):
-                nc.scalar.dma_start(
-                    out=sc_raw[32 * q : 32 * q + 4, :, :].bitcast(I32),
-                    in_=a_scales[:, 4 * q : 4 * q + 4, :].rearrange("k r n -> r k n").bitcast(I32),
+        def load_scales(queue, dst, c0, c1, quads=range(4)):
+            for q in quads:
+                queue.dma_start(
+                    out=dst[32 * q : 32 * q + 4, :, :].bitcast(I32),
+                    in_=a_scales[:, 4 * q : 4 * q + 4, c0:c1].rearrange("k r n -> r k n").bitcast(I32),
                 )
 
         def load_beta(g):
@@ -96,7 +101,7 @@ def tile_projection_pursuit_regression_s9_kernel(tc, x, a_words, a_scales, amp, 
 
         def transpose_x(mh, kp, half):
             ps = bank(4 + 2 * kp + half, [P, 2, 2, P], "x_ps%d%d%d" % (mh, kp, half))
-            words = x_raw[mh, kp, half][:].bitcast(F32)
+            words = x_raw[mh, kp, half].bitcast(F32)
             for a in range(2):
                 for u in range(2):
                     nc.tensor.transpose(ps[:, a, u, :], words[:, a, u : PASS // 2 : 2], ident[:])
@@ -124,9 +129,10 @@ def tile_projection_pursuit_regression_s9_kernel(tc, x, a_words, a_scales, amp, 
 
         def sort_scales(g):
             t = sb("a_sc%d" % g, [P, KP, PASS], U8)
+            src = sc_first[:] if g == 0 else sc_rest[:, :, PASS * (g - 1) : PASS * g]
             nc.vector.tensor_copy(
                 out=t[:].bitcast(I32).rearrange("p k (t j) -> p k t j", t=4),
-                in_=sc_raw[:, :, PASS * g : PASS * (g + 1)].bitcast(I32).rearrange("p k (j t) -> p k t j", t=4),
+                in_=src.bitcast(I32).rearrange("p k (j t) -> p k t j", t=4),
             )
             a_sc[g] = t
 
@@ -227,24 +233,25 @@ def tile_projection_pursuit_regression_s9_kernel(tc, x, a_words, a_scales, amp, 
                 nc.vector.tensor_tensor(out=y[:], in0=o_ps[mh, a][:, cols], in1=icpt[:, cols], op=ALU.add)
                 nc.sync.dma_start(out=out[r0 : r0 + P, cols], in_=y[:])
 
-        nc.vector.memset(sc_raw[:].bitcast(I32), 0)
+        nc.gpsimd.memset(amp_raw[:].bitcast(I32), 0)
+        nc.gpsimd.memset(sc_first[:].bitcast(I32), 0)
         make_identity(nc, ident[:])
-        nc.vector.memset(amp_rows[:], 0.0)
-        nc.sync.dma_start(out=amp_raw[:], in_=amp.rearrange("(g f) -> g f", g=G))
+        nc.vector.memset(sc_rest[:].bitcast(I32), 0)
         load_x(0, 0, 0)
         load_x(0, 0, 1)
+        nc.sync.dma_start(
+            out=amp_raw[0:P:32, :].rearrange("q (g c) -> q g c", g=G), in_=amp.rearrange("(g q c) -> q g c", g=G, q=4)
+        )
+        load_scales(nc.sync, sc_first, 0, PASS)
+        load_x(0, 1, 0, 2)
         load_a(0)
-        load_scales()
-        load_x(0, 1, 0)
-        load_x(0, 1, 1)
         load_lin(0)
+        load_scales(nc.sync, sc_rest, PASS, F)
         load_a(1)
         load_beta(0)
-        load_x(1, 0, 0)
-        load_x(1, 0, 1)
+        load_x(1, 0, 0, 2)
         load_a(2)
-        load_x(1, 1, 0)
-        load_x(1, 1, 1)
+        load_x(1, 1, 0, 2)
         load_a(3)
         load_beta(1)
         load_lin(1)
@@ -253,16 +260,13 @@ def tile_projection_pursuit_regression_s9_kernel(tc, x, a_words, a_scales, amp, 
         nc.sync.dma_start(out=icpt[:], in_=intercept.partition_broadcast(P))
 
         nc.vector.tensor_copy(
-            out=amp_rows[0:G, :, :].rearrange("g t (j i) -> g t j i", i=4),
-            in_=amp_raw[:].rearrange("g (j t i) -> g t j i", t=4, i=4),
+            out=amp_rows[:].rearrange("p (t g j i) -> p t g j i", t=4, g=G, i=4),
+            in_=amp_raw[:].rearrange("p (g j t i) -> p t g j i", t=4, g=G, i=4),
         )
-        amp_ps = bank(3, [P, 4, P], "amp_ps")
-        for t in range(4):
-            nc.tensor.transpose(amp_ps[:, t, :], amp_rows[:, t, :], ident[:])
-        for name in ("val", "mag", "guess", "inv", "neg", "quot", "sgn0", "halfroot"):
+        nc.vector.transpose(out=amp_cols[:], in_=amp_rows[:])
+        for name in ("mag", "guess", "inv", "neg", "quot", "sgn0", "halfroot"):
             small[name] = sb(name, [P, 4, G], F32)
-        val = small["val"][:]
-        nc.vector.tensor_copy(out=val, in_=amp_ps[:, :, 0:G])
+        val = amp_cols[:, 0:PASS:32].rearrange("p (t g) -> p t g", t=4)
         transpose_x(0, 0, 0)
         transpose_x(0, 0, 1)
         transpose_x(0, 1, 0)
@@ -270,10 +274,10 @@ def tile_projection_pursuit_regression_s9_kernel(tc, x, a_words, a_scales, amp, 
         nc.vector.scalar_tensor_tensor(out=small["mag"][:], in0=val, scalar=-1.0, in1=val, op0=ALU.mult, op1=ALU.max)
         nc.scalar.activation(out=small["guess"][:], in_=small["mag"][:], func=ACT.Sqrt, bias=TINY)
         copy_x(0, 0, 0, nc.vector.tensor_copy)
-        sort_a(0)
+        sort_scales(0)
         quant_x(0, 0, 0)
         copy_x(0, 0, 1, nc.vector.tensor_copy)
-        sort_scales(0)
+        sort_a(0)
         quant_x(0, 0, 1)
         copy_x(0, 1, 0, nc.scalar.copy)
         copy_x(0, 1, 1, nc.scalar.copy)
@@ -341,8 +345,8 @@ def tile_projection_pursuit_regression_s9_kernel(tc, x, a_words, a_scales, amp, 
         sign_beta(2)
         int_h(2)
         int_beta(2)
-        quant_h(2)
         quant_lin(1)
+        quant_h(2)
         quant_beta(2)
         ridges(1)
         trends(0, 1)
@@ -351,28 +355,31 @@ def tile_projection_pursuit_regression_s9_kernel(tc, x, a_words, a_scales, amp, 
         int_h(3)
         int_beta(3)
         quant_h(3)
-        int_h(4)
+        int_h(4, 0, 256)
         quant_beta(3)
+        int_h(4, 256, 512, nc.scalar.copy)
         ridges(2)
         z_group(6)
         ridges(3)
+        int_h(5, 0, 256)
+        int_h(5, 256, 512, nc.scalar.copy)
         quant_h(4)
-        int_h(5)
         z_group(7)
         finish(0, 0)
-        quant_h(5)
         finish(0, 1)
         finish(0, 2)
         finish(0, 3)
         int_h(6)
+        quant_h(5)
         trends(1, 0)
         trends(1, 1)
         ridges(4)
-        ridges(5)
-        int_h(7)
+        int_h(7, 0, 256, nc.scalar.copy)
+        int_h(7, 256, 512, nc.scalar.copy)
         quant_h(6)
-        quant_h(7)
+        quant_h(7, 0, 256)
+        quant_h(7, 256, 512)
         for a in range(4):
-            ridge(6, a)
-            ridge(7, a)
-            finish(1, a)
+            for s in (5, 6, 7):
+                ridge(s, a)
+            finish(1, a, 2 if a == 3 else 1)

from contextlib import ExitStack

import concourse.mybir as mybir
from concourse.masks import make_identity

M, K, F, R = 1024, 1024, 2048, 512
FLOPS = 2 * M * K * F + 2 * M * F * R + 2 * M * K * R

F32 = mybir.dt.float32
BF16 = mybir.dt.bfloat16
I32 = mybir.dt.int32
U32 = mybir.dt.uint32
U8 = mybir.dt.uint8
E4M3 = mybir.dt.float8_e4m3fn_x4
E5M2 = mybir.dt.float8_e5m2_x4
E2M1 = mybir.dt.float4_e2m1fn_x4
ALU = mybir.AluOpType
ACT = mybir.ActivationFunctionType

P = 128
PASS = 512
KP = K // PASS
G = F // PASS
HALF = 512
TINY = 2.0 ** -116


def tile_projection_pursuit_regression_s9_kernel(tc, x, a_words, a_scales, amp, beta, lin, intercept, out):
    nc = tc.nc
    with ExitStack() as ctx:
        keep = ctx.enter_context(tc.tile_pool(name="keep", bufs=1))
        psum = ctx.enter_context(tc.psum_pool(name="psum", bufs=1))
        ctx.enter_context(tc.manual_schedule())

        def sb(name, shape, dtype):
            return keep.tile(shape, dtype, name=name, tag=name, align_bytes=64)

        def staged(name):
            return keep.tile([P, 4 * HALF], BF16, name=name, tag="staged", bufs=3, align_bytes=64)

        def bank(b, shape, name):
            return psum.tile(shape, F32, name=name, tag="bank%d" % b)

        ident = sb("ident", [P, P], F32)
        sc_first = sb("sc_first", [P, KP, PASS], U8)
        sc_rest = sb("sc_rest", [P, KP, F - PASS], U8)
        amp_raw = sb("amp_raw", [P, PASS], BF16)
        amp_rows = sb("amp_rows", [P, PASS], BF16)
        amp_cols = sb("amp_cols", [P, PASS], BF16)
        icpt = sb("icpt", [P, R], BF16)
        root = sb("root", [P, 4, G], F32)
        sgn = sb("sgn", [P, 4, G], F32)

        x_raw, xq, xs = {}, {}, {}
        for mh in range(2):
            for kp in range(KP):
                xq[mh, kp] = sb("xq%d%d" % (mh, kp), [P, HALF], U32)
                xs[mh, kp] = sb("xs%d%d" % (mh, kp), [P, HALF], U8)
        a_raw, aq, a_sc = {}, {}, {}
        b_raw, b_int, bq, bs = {}, {}, {}, {}
        l_raw, l_int, lq, ls = {}, {}, {}, {}
        h_raw, h_int, hq, hs = {}, {}, {}, {}
        x_ps, x_int, z_ps, o_ps = {}, {}, {}, {}
        small = {}

        def load_x(mh, kp, half, halves=1):
            t = sb("x_raw%d%d%d" % (mh, kp, half), [P, 2 * halves, PASS], BF16)
            r0 = mh * HALF + half * 256
            nc.sync.dma_start(
                out=t[:], in_=x[r0 : r0 + 256 * halves, kp * PASS : (kp + 1) * PASS].rearrange("(a p) k -> p a k", p=P)
            )
            for n in range(halves):
                x_raw[mh, kp, half + n] = t[:, 2 * n : 2 * n + 2, :]

        def load_a(g):
            t = sb("a_raw%d" % g, [P, KP, 2 * PASS], U8)
            nc.sync.dma_start(
                out=t[:].bitcast(I32),
                in_=a_words[:, :, 2 * PASS * g : 2 * PASS * (g + 1)].rearrange("k p n -> p k n").bitcast(I32),
            )
            a_raw[g] = t

        def load_scales(queue, dst, c0, c1, quads=range(4)):
            for q in quads:
                queue.dma_start(
                    out=dst[32 * q : 32 * q + 4, :, :].bitcast(I32),
                    in_=a_scales[:, 4 * q : 4 * q + 4, c0:c1].rearrange("k r n -> r k n").bitcast(I32),
                )

        def load_beta(g):
            t = sb("b_raw%d" % g, [P, 4, R], BF16)
            rows = beta[g * PASS : (g + 1) * PASS, :].rearrange("(j t i) r -> i j t r", t=4, i=4)
            for i in range(4):
                nc.sync.dma_start(out=t[i:P:4, :, :], in_=rows[i])
            b_raw[g] = t

        def load_lin(kp):
            t = sb("l_raw%d" % kp, [P, 4, R], BF16)
            nc.sync.dma_start(out=t[:], in_=lin[kp * PASS : (kp + 1) * PASS, :].rearrange("(p t) r -> p t r", t=4))
            l_raw[kp] = t

        def transpose_x(mh, kp, half):
            ps = bank(4 + 2 * kp + half, [P, 2, 2, P], "x_ps%d%d%d" % (mh, kp, half))
            words = x_raw[mh, kp, half].bitcast(F32)
            for a in range(2):
                for u in range(2):
                    nc.tensor.transpose(ps[:, a, u, :], words[:, a, u : PASS // 2 : 2], ident[:])
            x_ps[mh, kp, half] = ps

        def copy_x(mh, kp, half, copy):
            t = sb("x_int%d%d%d" % (mh, kp, half), [P, 1024], BF16)
            copy(
                out=t[:].bitcast(F32).rearrange("p (a m u) -> p a m u", a=2, u=2),
                in_=x_ps[mh, kp, half][:].rearrange("p a u m -> p a m u"),
            )
            x_int[mh, kp, half] = t

        def quant_x(mh, kp, half):
            cols = slice(256 * half, 256 * (half + 1))
            nc.vector.quantize_mx(out=xq[mh, kp][:, cols].bitcast(E4M3), scales=xs[mh, kp][:, cols], in_=x_int[mh, kp, half][:])

        def sort_a(g):
            t = sb("aq%d" % g, [P, KP, 2 * PASS], U8)
            nc.vector.tensor_copy(
                out=t[:].bitcast(I32).rearrange("p k (t j w) -> p k t j w", t=4, w=2),
                in_=a_raw[g][:].bitcast(I32).rearrange("p k (j t w) -> p k t j w", t=4, w=2),
            )
            aq[g] = t

        def sort_scales(g):
            t = sb("a_sc%d" % g, [P, KP, PASS], U8)
            src = sc_first[:] if g == 0 else sc_rest[:, :, PASS * (g - 1) : PASS * g]
            nc.vector.tensor_copy(
                out=t[:].bitcast(I32).rearrange("p k (t j) -> p k t j", t=4),
                in_=src.bitcast(I32).rearrange("p k (j t) -> p k t j", t=4),
            )
            a_sc[g] = t

        def interleave(copy, dst, src, c0, c1):
            copy(
                out=dst[:, 4 * c0 : 4 * c1].rearrange("p (c i t) -> p c t i", i=4, t=4),
                in_=src[:, :, c0:c1].rearrange("p t (c i) -> p c t i", i=4),
            )

        def sign_beta(g):
            for t in range(4):
                nc.vector.tensor_scalar(b_raw[g][:, t, :], b_raw[g][:, t, :], sgn[:, t, g : g + 1], None, ALU.mult)

        def int_beta(g):
            b_int[g] = staged("b_int%d" % g)
            interleave(nc.vector.tensor_copy, b_int[g], b_raw[g], 0, R)

        def quant_beta(g):
            bq[g] = sb("bq%d" % g, [P, R], U32)
            bs[g] = sb("bs%d" % g, [P, R], U8)
            nc.vector.quantize_mx(out=bq[g][:].bitcast(E4M3), scales=bs[g][:], in_=b_int[g][:])

        def int_lin(kp, half):
            if half == 0:
                l_int[kp] = sb("l_int%d" % kp, [P, 4 * R], BF16)
            interleave(nc.scalar.copy, l_int[kp], l_raw[kp], 256 * half, 256 * (half + 1))

        def quant_lin(kp):
            lq[kp] = sb("lq%d" % kp, [P, R], U32)
            ls[kp] = sb("ls%d" % kp, [P, R], U8)
            nc.vector.quantize_mx(out=lq[kp][:].bitcast(E4M3), scales=ls[kp][:], in_=l_int[kp][:])

        def z_pass(s, t, kp):
            mh, g = divmod(s, G)
            if kp == 0:
                z_ps[s, t] = bank(t, [P, HALF], "z%d%d" % (s, t))
            nc.tensor.matmul_mx(
                out=z_ps[s, t][:],
                lhsT=aq[g][:, kp, 256 * t : 256 * (t + 1)].bitcast(E2M1),
                lhsT_scale=a_sc[g][:, kp, P * t : P * (t + 1)],
                rhs=xq[mh, kp][:].bitcast(E4M3),
                rhs_scale=xs[mh, kp][:],
                start=(kp == 0),
                stop=(kp == KP - 1),
            )

        def square(s, t):
            g = s % G
            if t == 0:
                h_raw[s] = sb("h_raw%d" % s, [P, 4, HALF], BF16)
            nc.scalar.activation(out=h_raw[s][:, t, :], in_=z_ps[s, t][:], func=ACT.Square, scale=root[:, t, g : g + 1])

        def z_group(s):
            for t in range(4):
                for kp in range(KP):
                    z_pass(s, t, kp)
                square(s, t)

        def int_h(s, c0=0, c1=HALF, copy=nc.vector.tensor_copy):
            if c0 == 0:
                h_int[s] = staged("h_int%d" % s)
            interleave(copy, h_int[s], h_raw[s], c0, c1)

        def quant_h(s, c0=0, c1=HALF):
            if c0 == 0:
                hq[s] = sb("hq%d" % s, [P, HALF], U32)
                hs[s] = sb("hs%d" % s, [P, HALF], U8)
            nc.vector.quantize_mx(out=hq[s][:, c0:c1].bitcast(E5M2), scales=hs[s][:, c0:c1], in_=h_int[s][:, 4 * c0 : 4 * c1])

        done = {}

        def out_pass(mh, a, lhs, lhs_scale, rhs, rhs_scale):
            n = done.get((mh, a), 0)
            if n == 0:
                o_ps[mh, a] = bank(4 + a, [P, R], "o%d%d" % (mh, a))
            nc.tensor.matmul_mx(
                out=o_ps[mh, a][:], lhsT=lhs, lhsT_scale=lhs_scale, rhs=rhs, rhs_scale=rhs_scale,
                start=(n == 0), stop=(n == KP + G - 1),
            )
            done[mh, a] = n + 1

        def ridge(s, a):
            mh, g = divmod(s, G)
            cols = slice(P * a, P * (a + 1))
            out_pass(mh, a, hq[s][:, cols].bitcast(E5M2), hs[s][:, cols], bq[g][:].bitcast(E4M3), bs[g][:])

        def trend(mh, a, kps=range(KP)):
            cols = slice(P * a, P * (a + 1))
            for kp in kps:
                out_pass(mh, a, xq[mh, kp][:, cols].bitcast(E4M3), xs[mh, kp][:, cols], lq[kp][:].bitcast(E4M3), ls[kp][:])

        def finish(mh, a, parts=1):
            r0 = mh * HALF + P * a
            w = R // parts
            for c in range(parts):
                y = sb("y%d%d%d" % (mh, a, c), [P, w], F32)
                cols = slice(w * c, w * (c + 1))
                nc.vector.tensor_tensor(out=y[:], in0=o_ps[mh, a][:, cols], in1=icpt[:, cols], op=ALU.add)
                nc.sync.dma_start(out=out[r0 : r0 + P, cols], in_=y[:])

        nc.gpsimd.memset(amp_raw[:].bitcast(I32), 0)
        nc.gpsimd.memset(sc_first[:].bitcast(I32), 0)
        make_identity(nc, ident[:])
        nc.vector.memset(sc_rest[:].bitcast(I32), 0)
        load_x(0, 0, 0)
        load_x(0, 0, 1)
        nc.sync.dma_start(
            out=amp_raw[0:P:32, :].rearrange("q (g c) -> q g c", g=G), in_=amp.rearrange("(g q c) -> q g c", g=G, q=4)
        )
        load_scales(nc.sync, sc_first, 0, PASS)
        load_x(0, 1, 0, 2)
        load_a(0)
        load_lin(0)
        load_scales(nc.sync, sc_rest, PASS, F)
        load_a(1)
        load_beta(0)
        load_x(1, 0, 0, 2)
        load_a(2)
        load_x(1, 1, 0, 2)
        load_a(3)
        load_beta(1)
        load_lin(1)
        load_beta(2)
        load_beta(3)
        nc.sync.dma_start(out=icpt[:], in_=intercept.partition_broadcast(P))

        nc.vector.tensor_copy(
            out=amp_rows[:].rearrange("p (t g j i) -> p t g j i", t=4, g=G, i=4),
            in_=amp_raw[:].rearrange("p (g j t i) -> p t g j i", t=4, g=G, i=4),
        )
        nc.vector.transpose(out=amp_cols[:], in_=amp_rows[:])
        for name in ("mag", "guess", "inv", "neg", "quot", "sgn0", "halfroot"):
            small[name] = sb(name, [P, 4, G], F32)
        val = amp_cols[:, 0:PASS:32].rearrange("p (t g) -> p t g", t=4)
        transpose_x(0, 0, 0)
        transpose_x(0, 0, 1)
        transpose_x(0, 1, 0)
        transpose_x(0, 1, 1)
        nc.vector.scalar_tensor_tensor(out=small["mag"][:], in0=val, scalar=-1.0, in1=val, op0=ALU.mult, op1=ALU.max)
        nc.scalar.activation(out=small["guess"][:], in_=small["mag"][:], func=ACT.Sqrt, bias=TINY)
        copy_x(0, 0, 0, nc.vector.tensor_copy)
        sort_scales(0)
        quant_x(0, 0, 0)
        copy_x(0, 0, 1, nc.vector.tensor_copy)
        sort_a(0)
        quant_x(0, 0, 1)
        copy_x(0, 1, 0, nc.scalar.copy)
        copy_x(0, 1, 1, nc.scalar.copy)
        nc.vector.tensor_scalar(small["neg"][:], val, 0.0, None, ALU.is_lt)
        nc.vector.reciprocal(out=small["inv"][:], in_=small["guess"][:])
        nc.vector.scalar_tensor_tensor(out=small["sgn0"][:], in0=val, scalar=0.0, in1=small["neg"][:], op0=ALU.is_gt, op1=ALU.subtract)
        nc.vector.scalar_tensor_tensor(out=small["quot"][:], in0=val, scalar=0.5, in1=small["inv"][:], op0=ALU.mult, op1=ALU.mult)
        nc.vector.scalar_tensor_tensor(out=small["halfroot"][:], in0=small["guess"][:], scalar=0.5, in1=small["sgn0"][:], op0=ALU.mult, op1=ALU.mult)
        quant_x(0, 1, 0)
        nc.vector.tensor_tensor(out=root[:], in0=small["halfroot"][:], in1=small["quot"][:], op=ALU.add)
        quant_x(0, 1, 1)
        nc.vector.tensor_scalar(sgn[:], small["neg"][:], -2.0, 1.0, ALU.mult, ALU.add)

        int_lin(0, 0)
        int_lin(0, 1)
        for t in range(4):
            z_pass(0, t, 0)
        for t in range(4):
            z_pass(0, t, 1)
            square(0, t)

        def ridges(s):
            for a in range(4):
                ridge(s, a)

        def trends(mh, kp):
            for a in range(4):
                trend(mh, a, [kp])

        sort_a(1)
        sort_scales(1)
        z_group(1)
        sign_beta(0)
        sort_scales(2)
        int_beta(0)
        sort_a(2)
        quant_beta(0)
        for half in range(2):
            transpose_x(1, 0, half)
            copy_x(1, 0, half, nc.scalar.copy)
        z_group(2)
        sort_scales(3)
        int_h(0)
        sort_a(3)
        quant_h(0)
        quant_lin(0)
        sign_beta(1)
        quant_x(1, 0, 0)
        quant_x(1, 0, 1)
        int_beta(1)
        for half in range(2):
            transpose_x(1, 1, half)
            copy_x(1, 1, half, nc.scalar.copy)
        z_group(3)
        int_h(1)
        quant_beta(1)
        quant_x(1, 1, 0)
        quant_x(1, 1, 1)
        quant_h(1)
        ridges(0)
        trends(0, 0)
        int_lin(1, 0)
        int_lin(1, 1)
        z_group(4)
        sign_beta(2)
        int_h(2)
        int_beta(2)
        quant_lin(1)
        quant_h(2)
        quant_beta(2)
        ridges(1)
        trends(0, 1)
        z_group(5)
        sign_beta(3)
        int_h(3)
        int_beta(3)
        quant_h(3)
        int_h(4, 0, 256)
        quant_beta(3)
        int_h(4, 256, 512, nc.scalar.copy)
        ridges(2)
        z_group(6)
        ridges(3)
        int_h(5, 0, 256)
        int_h(5, 256, 512, nc.scalar.copy)
        quant_h(4)
        z_group(7)
        finish(0, 0)
        finish(0, 1)
        finish(0, 2)
        finish(0, 3)
        int_h(6)
        quant_h(5)
        trends(1, 0)
        trends(1, 1)
        ridges(4)
        int_h(7, 0, 256, nc.scalar.copy)
        int_h(7, 256, 512, nc.scalar.copy)
        quant_h(6)
        quant_h(7, 0, 256)
        quant_h(7, 256, 512)
        for a in range(4):
            for s in (5, 6, 7):
                ridge(s, a)
            finish(1, a, 2 if a == 3 else 1)
